import numpy as np
import ml_dtypes


def mxq(x, axis, fmt="e4m3"):
    dtype, down = {"e4m3": (ml_dtypes.float8_e4m3fn, 7), "e5m2": (ml_dtypes.float8_e5m2, 14)}[fmt]
    v = np.moveaxis(np.asarray(x, np.float32).astype(ml_dtypes.bfloat16).astype(np.float64), axis, -1)
    blocks = v.reshape(v.shape[:-1] + (-1, 32))
    amax = np.abs(blocks).max(-1, keepdims=True)
    byte = np.maximum(np.where(amax > 0, np.frexp(amax)[1] - 1 + 127, 0) - down, 1)
    scale = np.exp2(byte - 127.0)
    codes = (blocks / scale).astype(np.float32).astype(dtype).astype(np.float64)
    return np.moveaxis((codes * scale).reshape(v.shape), -1, axis)


WIDE = False


def mx_kscale(k):
    if not WIDE:
        return np.ones(k)
    levels = np.array([10, -10, 5, -5, 0])
    if k % 512:
        return np.exp2(np.random.permutation(np.resize(levels, k // 32))).repeat(32)
    a = np.empty((k // 512, 16))
    for p in range(k // 512):
        a[p, :8] = np.random.permutation(np.resize(levels, 8))
        for g in range(8):
            far = levels[np.abs(levels - a[p, g]) >= 10]
            a[p, g + 8] = far[np.random.randint(len(far))]
    return np.exp2(a.ravel()).repeat(32)


def f64(x):
    return np.asarray(x).astype(np.float64)


def striped8(idx):
    return np.asarray(idx).reshape(8, -1, 16).transpose(0, 2, 1).reshape(128, -1).astype(np.uint16)


def unstriped8(offs):
    return offs.reshape(8, 16, -1).transpose(0, 2, 1).reshape(8, -1).astype(np.int64)


def pick8(x, idx, run):
    r = np.arange(len(x))
    return x[r[:, None], idx[r % (8 * run) // run]]


E2M1 = np.array([0.0, 0.5, 1.0, 1.5, 2.0, 3.0, 4.0, 6.0, -0.0, -0.5, -1.0, -1.5, -2.0, -3.0, -4.0, -6.0])


def pack_weight(w, fmt):
    k, n = w.shape
    w = f64(np.asarray(w, np.float32).astype(ml_dtypes.bfloat16)).reshape(k // 32, 32, n)
    amax = np.abs(w).max(1)
    if fmt == "e4m3":
        byte = np.frexp(amax)[1] - 1 + 127 - 7
    else:
        mant, ex = np.frexp(amax / 6.0)
        byte = np.where(mant > 0.5, ex, ex - 1) + 127
    byte = np.clip(np.where(amax > 0, byte, 1), 1, 254)
    scaled = (w * np.exp2(127.0 - byte)[:, None, :]).reshape(k, n).astype(np.float32)
    by_word = np.ascontiguousarray(scaled.reshape(k // 512, 128, 4, n).transpose(0, 1, 3, 2))
    if fmt == "e4m3":
        words = by_word.astype(ml_dtypes.float8_e4m3fn).view(np.uint8)
    else:
        c = by_word.astype(ml_dtypes.float4_e2m1fn).view(np.uint8) & 0xF
        words = (c[..., 0::2] | (c[..., 1::2] << 4)).reshape(k // 512, 128, 2 * n)
    return np.ascontiguousarray(words), np.ascontiguousarray(byte.astype(np.uint8).reshape(k // 512, 16, n))


def unpack_weight(words, scales, fmt):
    g, _, n = scales.shape
    words = np.ascontiguousarray(words).reshape(g, 128, n, -1)
    if fmt == "e4m3":
        vals = words.view(ml_dtypes.float8_e4m3fn).astype(np.float64)
    else:
        nib = np.empty((g, 128, n, 4), np.uint8)
        nib[..., 0::2] = words & 0xF
        nib[..., 1::2] = words >> 4
        vals = E2M1[nib]
    vals = vals * np.repeat(np.exp2(scales.astype(np.float64) - 127.0), 8, axis=1)[..., None]
    return vals.transpose(0, 1, 3, 2).reshape(g * 512, n)


D, T, I, Q = 512, 1024, 512, 128


def setup_inputs():
    n = np.random.standard_normal
    idx = np.stack([np.random.permutation(T)[:I] for _ in range(8)])
    idx2 = np.stack([np.random.permutation(T)[:I] for _ in range(8)])
    idx3 = np.stack([np.random.permutation(T)[:I] for _ in range(8)])
    fd = mx_kscale(D)
    keysp = pack_weight(n((D, T)) / fd[:, None], "e2m1")
    return {
        "query": (n((D, Q)) * 0.9 / np.sqrt(D) * fd[:, None]).astype(np.float32),
        "query2": (n((D, Q)) * 0.9 / np.sqrt(D) * fd[:, None]).astype(np.float32),
        "keys_words": keysp[0],
        "keys_scales": keysp[1],
        "lam": (np.random.uniform(0.8, 1.6, (Q, 1))).astype(np.float32),
        "old": (1.0 * n((Q, T))).astype(np.float32),
        "offs": striped8(idx),
        "offs2": striped8(idx2),
        "offs3": striped8(idx3),
    }


def reference(query, query2, keys_words, keys_scales, lam, old, offs, offs2, offs3):
    idx = unstriped8(offs)
    idx2 = unstriped8(offs2)
    idx3 = unstriped8(offs3)
    keysu = unpack_weight(keys_words, keys_scales, "e2m1")
    queryq = mxq(f64(query), 0, "e4m3")
    a = queryq.T @ keysu
    query2q = mxq(f64(query2), 0, "e4m3")
    b = query2q.T @ keysu
    w = np.log(np.exp(pick8(a, idx, 16)) + np.exp(pick8(b, idx2, 16))) * f64(lam)
    f1 = np.zeros((Q, T))
    f1[np.arange(Q)[:, None], idx3[np.arange(Q) % 128 // 16]] = w
    y = f64(old) + f1
    return y

@@ -1,0 +1,124 @@
+import math
+from contextlib import ExitStack
+
+import concourse.mybir as mybir
+
+D, T, I, Q = 512, 1024, 512, 128
+FLOPS = 2 * 2 * D * T * Q
+
+F32 = mybir.dt.float32
+BF16 = mybir.dt.bfloat16
+I32 = mybir.dt.int32
+U32 = mybir.dt.uint32
+U16 = mybir.dt.uint16
+U8 = mybir.dt.uint8
+FP8X4 = mybir.dt.float8_e4m3fn_x4
+FP4X4 = mybir.dt.float4_e2m1fn_x4
+ALU = mybir.AluOpType
+ACT = mybir.ActivationFunctionType
+
+P = 128
+PACK = 4
+N_PASS = 256
+HALF = I // 2
+STORE = 256
+CAP = 2.0**40
+LOG_CAP = math.log(CAP)
+
+
+def tile_attend_eithertoken_lean_putold_heads_kernel(
+    tc, query, query2, keys_words, keys_scales, lam, old, offs, offs2, offs3, out
+):
+    nc = tc.nc
+    with ExitStack() as ctx:
+        sb = ctx.enter_context(tc.tile_pool(name="sb", bufs=1))
+        ps = ctx.enter_context(tc.psum_pool(name="ps", bufs=1))
+
+        key_words = sb.tile([P, 2 * T], U8, name="key_words", align_bytes=64)
+        key_scales = sb.tile([P, T], U8, name="key_scales", align_bytes=64)
+        raw_b = sb.tile([P, PACK, Q], F32, name="raw_b")
+        raw_a = sb.tile([P, PACK, Q], F32, name="raw_a")
+        list_a = sb.tile([P, I // 16], U16, name="list_a")
+        list_b = sb.tile([P, I // 16], U16, name="list_b")
+        list_put = sb.tile([P, I // 16], U16, name="list_put")
+        lam_col = sb.tile([P, 1], F32, name="lam_col")
+        old_sb = sb.tile([P, T], F32, name="old_sb")
+        placed = sb.tile([P, T], F32, name="placed")
+
+        nc.vector.memset(key_scales[:].bitcast(I32), 0)
+        nc.sync.dma_start(out=raw_b[:], in_=query2.rearrange("(p j) q -> p j q", j=PACK))
+        nc.sync.dma_start(out=key_words[:].bitcast(I32), in_=keys_words[0].bitcast(I32))
+        nc.sync.dma_start(out=raw_a[:], in_=query.rearrange("(p j) q -> p j q", j=PACK))
+        for quad in range(4):
+            nc.scalar.dma_start(
+                out=key_scales[32 * quad : 32 * quad + 4, :].bitcast(I32),
+                in_=keys_scales[0, 4 * quad : 4 * quad + 4, :].bitcast(I32),
+            )
+        nc.sync.dma_start(list_b[:], offs2)
+        nc.sync.dma_start(list_a[:], offs)
+        nc.sync.dma_start(out=lam_col[:], in_=lam)
+        nc.sync.dma_start(list_put[:], offs3)
+        nc.sync.dma_start(out=old_sb[:], in_=old)
+        nc.vector.memset(placed[:], 0.0)
+
+        def scores(name, raw, copy_out):
+            grouped = sb.tile([P, Q, PACK], BF16, name=name + "_grouped", align_bytes=64)
+            codes = sb.tile([P, Q], U32, name=name + "_codes", align_bytes=64)
+            scales = sb.tile([P, Q], U8, name=name + "_scales", align_bytes=64)
+            result = sb.tile([P, T], F32, name=name)
+            nc.vector.tensor_copy(out=grouped[:], in_=raw[:].rearrange("p j q -> p q j"))
+            nc.vector.quantize_mx(
+                out=codes[:].bitcast(FP8X4), scales=scales[:], in_=grouped[:].rearrange("p q j -> p (q j)")
+            )
+            for n0 in range(0, T, N_PASS):
+                bank = ps.tile([P, 512], F32, name="%s_bank%d" % (name, n0))
+                nc.tensor.matmul_mx(
+                    out=bank[:, 0:N_PASS],
+                    lhsT=codes[:].bitcast(FP8X4),
+                    lhsT_scale=scales[:],
+                    rhs=key_words[:, 2 * n0 : 2 * (n0 + N_PASS)].bitcast(FP4X4),
+                    rhs_scale=key_scales[:, n0 : n0 + N_PASS],
+                    start=True,
+                    stop=True,
+                )
+                copy_out(result[:, n0 : n0 + N_PASS], bank[:, 0:N_PASS])
+            return result
+
+        b = scores("b", raw_b, nc.scalar.copy)
+        a = scores("a", raw_a, nc.vector.tensor_copy)
+
+        slots = [slice(0, HALF), slice(HALF, I)]
+        cols = [slice(0, HALF // 16), slice(HALF // 16, I // 16)]
+        y = sb.tile([P, I], F32, name="y")
+        x_late = sb.tile([P, HALF], F32, name="x_late")
+        d = sb.tile([P, I], F32, name="d")
+        e = sb.tile([P, I], F32, name="e")
+        capped = sb.tile([P, I], F32, name="capped")
+        soft = sb.tile([P, I], F32, name="soft")
+        soft_lam = sb.tile([P, I], F32, name="soft_lam")
+        base = sb.tile([P, I], F32, name="base")
+        base_lam = sb.tile([P, I], F32, name="base_lam")
+
+        for h in range(2):
+            nc.scalar.activation(y[:, slots[h]], b[:].indirect(list_b[:, cols[h]]), ACT.Copy)
+        nc.vector.tensor_tensor(d[:, slots[0]], a[:].indirect(list_a[:, cols[0]]), y[:, slots[0]], ALU.subtract)
+        nc.scalar.activation(x_late[:], a[:].indirect(list_a[:, cols[1]]), ACT.Copy)
+        nc.vector.tensor_tensor(d[:, slots[1]], x_late[:], y[:, slots[1]], ALU.subtract)
+        for h in range(2):
+            nc.scalar.activation(e[:, slots[h]], d[:, slots[h]], ACT.Exp)
+        for h in range(2):
+            nc.vector.tensor_scalar(capped[:, slots[h]], e[:, slots[h]], CAP, 1.0, ALU.min, ALU.add)
+        nc.vector.scalar_tensor_tensor(base[:], d[:], LOG_CAP, y[:], ALU.max, ALU.add)
+        nc.vector.tensor_scalar(base_lam[:], base[:], -LOG_CAP, lam_col[:], ALU.add, ALU.mult)
+        for h in range(2):
+            nc.scalar.activation(soft[:, slots[h]], capped[:, slots[h]], ACT.Ln)
+            nc.scalar.activation(soft_lam[:, slots[h]], soft[:, slots[h]], ACT.Copy, scale=lam_col[:])
+            nc.vector.tensor_tensor(
+                placed[:].indirect(list_put[:, cols[h]]), base_lam[:, slots[h]], soft_lam[:, slots[h]], ALU.add
+            )
+
+        for s, n0 in enumerate(range(0, T, STORE)):
+            total = sb.tile([P, STORE], F32, name="total%d" % s)
+            nc.vector.tensor_tensor(total[:], placed[:, n0 : n0 + STORE], old_sb[:, n0 : n0 + STORE], ALU.add)
+            queue = nc.sync if s % 2 == 0 else nc.scalar
+            queue.dma_start(out=out[:, n0 : n0 + STORE], in_=total[:])

@@ -21,7 +21,7 @@ P = 128
 PACK = 4
 N_PASS = 256
 HALF = I // 2
-STORE = 256
+STORES = [0, 320, 640, 896, T]
 CAP = 2.0**40
 LOG_CAP = math.log(CAP)
 
@@ -45,7 +45,6 @@ def tile_attend_eithertoken_lean_putold_heads_kernel(
         old_sb = sb.tile([P, T], F32, name="old_sb")
         placed = sb.tile([P, T], F32, name="placed")
 
-        nc.vector.memset(key_scales[:].bitcast(I32), 0)
         nc.sync.dma_start(out=raw_b[:], in_=query2.rearrange("(p j) q -> p j q", j=PACK))
         nc.sync.dma_start(out=key_words[:].bitcast(I32), in_=keys_words[0].bitcast(I32))
         nc.sync.dma_start(out=raw_a[:], in_=query.rearrange("(p j) q -> p j q", j=PACK))
@@ -61,16 +60,17 @@ def tile_attend_eithertoken_lean_putold_heads_kernel(
         nc.sync.dma_start(out=old_sb[:], in_=old)
         nc.vector.memset(placed[:], 0.0)
 
-        def scores(name, raw, copy_out):
+        def scores(name, raw, casts, copies):
             grouped = sb.tile([P, Q, PACK], BF16, name=name + "_grouped", align_bytes=64)
             codes = sb.tile([P, Q], U32, name=name + "_codes", align_bytes=64)
             scales = sb.tile([P, Q], U8, name=name + "_scales", align_bytes=64)
-            result = sb.tile([P, T], F32, name=name)
-            nc.vector.tensor_copy(out=grouped[:], in_=raw[:].rearrange("p j q -> p q j"))
+            result = sb.tile([P, T], F32, name=name, tag=name)
+            for cast, q0, q1 in casts:
+                cast(out=grouped[:, q0:q1, :], in_=raw[:, :, q0:q1].rearrange("p j q -> p q j"))
             nc.vector.quantize_mx(
                 out=codes[:].bitcast(FP8X4), scales=scales[:], in_=grouped[:].rearrange("p q j -> p (q j)")
             )
-            for n0 in range(0, T, N_PASS):
+            for copy_out, n0 in zip(copies, range(0, T, N_PASS)):
                 bank = ps.tile([P, 512], F32, name="%s_bank%d" % (name, n0))
                 nc.tensor.matmul_mx(
                     out=bank[:, 0:N_PASS],
@@ -84,17 +84,16 @@ def tile_attend_eithertoken_lean_putold_heads_kernel(
                 copy_out(result[:, n0 : n0 + N_PASS], bank[:, 0:N_PASS])
             return result
 
-        b = scores("b", raw_b, nc.scalar.copy)
-        a = scores("a", raw_a, nc.vector.tensor_copy)
+        b = scores("b", raw_b, [(nc.vector.tensor_copy, 0, 80), (nc.scalar.copy, 80, Q)], [nc.scalar.copy, nc.scalar.copy, nc.vector.tensor_copy, nc.scalar.copy])
+        a = scores("a", raw_a, [(nc.vector.tensor_copy, 0, Q)], [nc.vector.tensor_copy] * 4)
 
         slots = [slice(0, HALF), slice(HALF, I)]
         cols = [slice(0, HALF // 16), slice(HALF // 16, I // 16)]
         y = sb.tile([P, I], F32, name="y")
-        x_late = sb.tile([P, HALF], F32, name="x_late")
         d = sb.tile([P, I], F32, name="d")
         e = sb.tile([P, I], F32, name="e")
         capped = sb.tile([P, I], F32, name="capped")
-        soft = sb.tile([P, I], F32, name="soft")
+        soft = sb.tile([P, HALF], F32, name="soft")
         soft_lam = sb.tile([P, I], F32, name="soft_lam")
         base = sb.tile([P, I], F32, name="base")
         base_lam = sb.tile([P, I], F32, name="base_lam")
@@ -102,6 +101,7 @@ def tile_attend_eithertoken_lean_putold_heads_kernel(
         for h in range(2):
             nc.scalar.activation(y[:, slots[h]], b[:].indirect(list_b[:, cols[h]]), ACT.Copy)
         nc.vector.tensor_tensor(d[:, slots[0]], a[:].indirect(list_a[:, cols[0]]), y[:, slots[0]], ALU.subtract)
+        x_late = sb.tile([P, HALF], F32, name="x_late", tag="b")
         nc.scalar.activation(x_late[:], a[:].indirect(list_a[:, cols[1]]), ACT.Copy)
         nc.vector.tensor_tensor(d[:, slots[1]], x_late[:], y[:, slots[1]], ALU.subtract)
         for h in range(2):
@@ -111,14 +111,15 @@ def tile_attend_eithertoken_lean_putold_heads_kernel(
         nc.vector.scalar_tensor_tensor(base[:], d[:], LOG_CAP, y[:], ALU.max, ALU.add)
         nc.vector.tensor_scalar(base_lam[:], base[:], -LOG_CAP, lam_col[:], ALU.add, ALU.mult)
         for h in range(2):
-            nc.scalar.activation(soft[:, slots[h]], capped[:, slots[h]], ACT.Ln)
-            nc.scalar.activation(soft_lam[:, slots[h]], soft[:, slots[h]], ACT.Copy, scale=lam_col[:])
+            nc.scalar.activation(soft[:], capped[:, slots[h]], ACT.Ln)
+            nc.scalar.activation(soft_lam[:, slots[h]], soft[:], ACT.Copy, scale=lam_col[:])
             nc.vector.tensor_tensor(
                 placed[:].indirect(list_put[:, cols[h]]), base_lam[:, slots[h]], soft_lam[:, slots[h]], ALU.add
             )
 
-        for s, n0 in enumerate(range(0, T, STORE)):
-            total = sb.tile([P, STORE], F32, name="total%d" % s)
-            nc.vector.tensor_tensor(total[:], placed[:, n0 : n0 + STORE], old_sb[:, n0 : n0 + STORE], ALU.add)
+        for s in range(len(STORES) - 1):
+            part = slice(STORES[s], STORES[s + 1])
+            total = sb.tile([P, STORES[s + 1] - STORES[s]], F32, name="total%d" % s)
+            nc.vector.tensor_tensor(total[:], placed[:, part], old_sb[:, part], ALU.add)
             queue = nc.sync if s % 2 == 0 else nc.scalar
-            queue.dma_start(out=out[:, n0 : n0 + STORE], in_=total[:])
+            queue.dma_start(out=out[:, part], in_=total[:])

@@ -21,7 +21,7 @@ P = 128
 PACK = 4
 N_PASS = 256
 HALF = I // 2
-STORES = [0, 320, 640, 896, T]
+STORES = [0, 256, 512, 768, T]
 CAP = 2.0**40
 LOG_CAP = math.log(CAP)
 
@@ -61,15 +61,17 @@ def tile_attend_eithertoken_lean_putold_heads_kernel(
         nc.vector.memset(placed[:], 0.0)
 
         def scores(name, raw, casts, copies):
-            grouped = sb.tile([P, Q, PACK], BF16, name=name + "_grouped", align_bytes=64)
             codes = sb.tile([P, Q], U32, name=name + "_codes", align_bytes=64)
             scales = sb.tile([P, Q], U8, name=name + "_scales", align_bytes=64)
             result = sb.tile([P, T], F32, name=name, tag=name)
             for cast, q0, q1 in casts:
-                cast(out=grouped[:, q0:q1, :], in_=raw[:, :, q0:q1].rearrange("p j q -> p q j"))
-            nc.vector.quantize_mx(
-                out=codes[:].bitcast(FP8X4), scales=scales[:], in_=grouped[:].rearrange("p q j -> p (q j)")
-            )
+                grouped = sb.tile([P, q1 - q0, PACK], BF16, name="%s_grouped%d" % (name, q0), align_bytes=64)
+                cast(out=grouped[:], in_=raw[:, :, q0:q1].rearrange("p j q -> p q j"))
+                nc.vector.quantize_mx(
+                    out=codes[:, q0:q1].bitcast(FP8X4),
+                    scales=scales[:, q0:q1],
+                    in_=grouped[:].rearrange("p q j -> p (q j)"),
+                )
             for copy_out, n0 in zip(copies, range(0, T, N_PASS)):
                 bank = ps.tile([P, 512], F32, name="%s_bank%d" % (name, n0))
                 nc.tensor.matmul_mx(
@@ -84,7 +86,7 @@ def tile_attend_eithertoken_lean_putold_heads_kernel(
                 copy_out(result[:, n0 : n0 + N_PASS], bank[:, 0:N_PASS])
             return result
 
-        b = scores("b", raw_b, [(nc.vector.tensor_copy, 0, 80), (nc.scalar.copy, 80, Q)], [nc.scalar.copy, nc.scalar.copy, nc.vector.tensor_copy, nc.scalar.copy])
+        b = scores("b", raw_b, [(nc.vector.tensor_copy, 0, 64), (nc.vector.tensor_copy, 64, Q)], [nc.scalar.copy, nc.scalar.copy, nc.vector.tensor_copy, nc.scalar.copy])
         a = scores("a", raw_a, [(nc.vector.tensor_copy, 0, Q)], [nc.vector.tensor_copy] * 4)
 
         slots = [slice(0, HALF), slice(HALF, I)]
@@ -100,10 +102,8 @@ def tile_attend_eithertoken_lean_putold_heads_kernel(
 
         for h in range(2):
             nc.scalar.activation(y[:, slots[h]], b[:].indirect(list_b[:, cols[h]]), ACT.Copy)
-        nc.vector.tensor_tensor(d[:, slots[0]], a[:].indirect(list_a[:, cols[0]]), y[:, slots[0]], ALU.subtract)
-        x_late = sb.tile([P, HALF], F32, name="x_late", tag="b")
-        nc.scalar.activation(x_late[:], a[:].indirect(list_a[:, cols[1]]), ACT.Copy)
-        nc.vector.tensor_tensor(d[:, slots[1]], x_late[:], y[:, slots[1]], ALU.subtract)
+        for h in range(2):
+            nc.vector.tensor_tensor(d[:, slots[h]], a[:].indirect(list_a[:, cols[h]]), y[:, slots[h]], ALU.subtract)
         for h in range(2):
             nc.scalar.activation(e[:, slots[h]], d[:, slots[h]], ACT.Exp)
         for h in range(2):
@@ -111,8 +111,12 @@ def tile_attend_eithertoken_lean_putold_heads_kernel(
         nc.vector.scalar_tensor_tensor(base[:], d[:], LOG_CAP, y[:], ALU.max, ALU.add)
         nc.vector.tensor_scalar(base_lam[:], base[:], -LOG_CAP, lam_col[:], ALU.add, ALU.mult)
         for h in range(2):
-            nc.scalar.activation(soft[:], capped[:, slots[h]], ACT.Ln)
-            nc.scalar.activation(soft_lam[:, slots[h]], soft[:], ACT.Copy, scale=lam_col[:])
+            for u in range(2):
+                piece = slice(u * HALF // 2, (u + 1) * HALF // 2)
+                nc.scalar.activation(soft[:, piece], capped[:, slots[h]][:, piece], ACT.Ln)
+            for u in range(2):
+                piece = slice(u * HALF // 2, (u + 1) * HALF // 2)
+                nc.scalar.activation(soft_lam[:, slots[h]][:, piece], soft[:, piece], ACT.Copy, scale=lam_col[:])
             nc.vector.tensor_tensor(
                 placed[:].indirect(list_put[:, cols[h]]), base_lam[:, slots[h]], soft_lam[:, slots[h]], ALU.add
             )

@@ -95,7 +95,7 @@ def tile_attend_eithertoken_lean_putold_heads_kernel(
         d = sb.tile([P, I], F32, name="d")
         e = sb.tile([P, I], F32, name="e")
         capped = sb.tile([P, I], F32, name="capped")
-        soft = sb.tile([P, HALF], F32, name="soft")
+        soft = sb.tile([P, I], F32, name="soft")
         soft_lam = sb.tile([P, I], F32, name="soft_lam")
         base = sb.tile([P, I], F32, name="base")
         base_lam = sb.tile([P, I], F32, name="base_lam")
@@ -111,15 +111,11 @@ def tile_attend_eithertoken_lean_putold_heads_kernel(
         nc.vector.scalar_tensor_tensor(base[:], d[:], LOG_CAP, y[:], ALU.max, ALU.add)
         nc.vector.tensor_scalar(base_lam[:], base[:], -LOG_CAP, lam_col[:], ALU.add, ALU.mult)
         for h in range(2):
-            for u in range(2):
-                piece = slice(u * HALF // 2, (u + 1) * HALF // 2)
-                nc.scalar.activation(soft[:, piece], capped[:, slots[h]][:, piece], ACT.Ln)
-            for u in range(2):
-                piece = slice(u * HALF // 2, (u + 1) * HALF // 2)
-                nc.scalar.activation(soft_lam[:, slots[h]][:, piece], soft[:, piece], ACT.Copy, scale=lam_col[:])
-            nc.vector.tensor_tensor(
-                placed[:].indirect(list_put[:, cols[h]]), base_lam[:, slots[h]], soft_lam[:, slots[h]], ALU.add
+            nc.scalar.activation(soft[:, slots[h]], capped[:, slots[h]], ACT.Ln)
+            nc.vector.scalar_tensor_tensor(
+                soft_lam[:, slots[h]], soft[:, slots[h]], lam_col[:], base_lam[:, slots[h]], ALU.mult, ALU.add
             )
+            nc.vector.tensor_copy(placed[:].indirect(list_put[:, cols[h]]), soft_lam[:, slots[h]])
 
         for s in range(len(STORES) - 1):
             part = slice(STORES[s], STORES[s + 1])

import math
from contextlib import ExitStack

import concourse.mybir as mybir

D, T, I, Q = 512, 1024, 512, 128
FLOPS = 2 * 2 * D * T * Q

F32 = mybir.dt.float32
BF16 = mybir.dt.bfloat16
I32 = mybir.dt.int32
U32 = mybir.dt.uint32
U16 = mybir.dt.uint16
U8 = mybir.dt.uint8
FP8X4 = mybir.dt.float8_e4m3fn_x4
FP4X4 = mybir.dt.float4_e2m1fn_x4
ALU = mybir.AluOpType
ACT = mybir.ActivationFunctionType

P = 128
PACK = 4
N_PASS = 256
HALF = I // 2
STORES = [0, 256, 512, 768, T]
CAP = 2.0**40
LOG_CAP = math.log(CAP)


def tile_attend_eithertoken_lean_putold_heads_kernel(
    tc, query, query2, keys_words, keys_scales, lam, old, offs, offs2, offs3, out
):
    nc = tc.nc
    with ExitStack() as ctx:
        sb = ctx.enter_context(tc.tile_pool(name="sb", bufs=1))
        ps = ctx.enter_context(tc.psum_pool(name="ps", bufs=1))

        key_words = sb.tile([P, 2 * T], U8, name="key_words", align_bytes=64)
        key_scales = sb.tile([P, T], U8, name="key_scales", align_bytes=64)
        raw_b = sb.tile([P, PACK, Q], F32, name="raw_b")
        raw_a = sb.tile([P, PACK, Q], F32, name="raw_a")
        list_a = sb.tile([P, I // 16], U16, name="list_a")
        list_b = sb.tile([P, I // 16], U16, name="list_b")
        list_put = sb.tile([P, I // 16], U16, name="list_put")
        lam_col = sb.tile([P, 1], F32, name="lam_col")
        old_sb = sb.tile([P, T], F32, name="old_sb")
        placed = sb.tile([P, T], F32, name="placed")

        nc.sync.dma_start(out=raw_b[:], in_=query2.rearrange("(p j) q -> p j q", j=PACK))
        nc.sync.dma_start(out=key_words[:].bitcast(I32), in_=keys_words[0].bitcast(I32))
        nc.sync.dma_start(out=raw_a[:], in_=query.rearrange("(p j) q -> p j q", j=PACK))
        for quad in range(4):
            nc.scalar.dma_start(
                out=key_scales[32 * quad : 32 * quad + 4, :].bitcast(I32),
                in_=keys_scales[0, 4 * quad : 4 * quad + 4, :].bitcast(I32),
            )
        nc.sync.dma_start(list_b[:], offs2)
        nc.sync.dma_start(list_a[:], offs)
        nc.sync.dma_start(out=lam_col[:], in_=lam)
        nc.sync.dma_start(list_put[:], offs3)
        nc.sync.dma_start(out=old_sb[:], in_=old)
        nc.vector.memset(placed[:], 0.0)

        def scores(name, raw, casts, copies):
            codes = sb.tile([P, Q], U32, name=name + "_codes", align_bytes=64)
            scales = sb.tile([P, Q], U8, name=name + "_scales", align_bytes=64)
            result = sb.tile([P, T], F32, name=name, tag=name)
            for cast, q0, q1 in casts:
                grouped = sb.tile([P, q1 - q0, PACK], BF16, name="%s_grouped%d" % (name, q0), align_bytes=64)
                cast(out=grouped[:], in_=raw[:, :, q0:q1].rearrange("p j q -> p q j"))
                nc.vector.quantize_mx(
                    out=codes[:, q0:q1].bitcast(FP8X4),
                    scales=scales[:, q0:q1],
                    in_=grouped[:].rearrange("p q j -> p (q j)"),
                )
            for copy_out, n0 in zip(copies, range(0, T, N_PASS)):
                bank = ps.tile([P, 512], F32, name="%s_bank%d" % (name, n0))
                nc.tensor.matmul_mx(
                    out=bank[:, 0:N_PASS],
                    lhsT=codes[:].bitcast(FP8X4),
                    lhsT_scale=scales[:],
                    rhs=key_words[:, 2 * n0 : 2 * (n0 + N_PASS)].bitcast(FP4X4),
                    rhs_scale=key_scales[:, n0 : n0 + N_PASS],
                    start=True,
                    stop=True,
                )
                copy_out(result[:, n0 : n0 + N_PASS], bank[:, 0:N_PASS])
            return result

        b = scores("b", raw_b, [(nc.vector.tensor_copy, 0, 64), (nc.vector.tensor_copy, 64, Q)], [nc.scalar.copy, nc.scalar.copy, nc.vector.tensor_copy, nc.scalar.copy])
        a = scores("a", raw_a, [(nc.vector.tensor_copy, 0, Q)], [nc.vector.tensor_copy] * 4)

        slots = [slice(0, HALF), slice(HALF, I)]
        cols = [slice(0, HALF // 16), slice(HALF // 16, I // 16)]
        y = sb.tile([P, I], F32, name="y")
        d = sb.tile([P, I], F32, name="d")
        e = sb.tile([P, I], F32, name="e")
        capped = sb.tile([P, I], F32, name="capped")
        soft = sb.tile([P, I], F32, name="soft")
        soft_lam = sb.tile([P, I], F32, name="soft_lam")
        base = sb.tile([P, I], F32, name="base")
        base_lam = sb.tile([P, I], F32, name="base_lam")

        for h in range(2):
            nc.scalar.activation(y[:, slots[h]], b[:].indirect(list_b[:, cols[h]]), ACT.Copy)
        for h in range(2):
            nc.vector.tensor_tensor(d[:, slots[h]], a[:].indirect(list_a[:, cols[h]]), y[:, slots[h]], ALU.subtract)
        for h in range(2):
            nc.scalar.activation(e[:, slots[h]], d[:, slots[h]], ACT.Exp)
        for h in range(2):
            nc.vector.tensor_scalar(capped[:, slots[h]], e[:, slots[h]], CAP, 1.0, ALU.min, ALU.add)
        nc.vector.scalar_tensor_tensor(base[:], d[:], LOG_CAP, y[:], ALU.max, ALU.add)
        nc.vector.tensor_scalar(base_lam[:], base[:], -LOG_CAP, lam_col[:], ALU.add, ALU.mult)
        for h in range(2):
            nc.scalar.activation(soft[:, slots[h]], capped[:, slots[h]], ACT.Ln)
            nc.vector.scalar_tensor_tensor(
                soft_lam[:, slots[h]], soft[:, slots[h]], lam_col[:], base_lam[:, slots[h]], ALU.mult, ALU.add
            )
            nc.vector.tensor_copy(placed[:].indirect(list_put[:, cols[h]]), soft_lam[:, slots[h]])

        for s in range(len(STORES) - 1):
            part = slice(STORES[s], STORES[s + 1])
            total = sb.tile([P, STORES[s + 1] - STORES[s]], F32, name="total%d" % s)
            nc.vector.tensor_tensor(total[:], placed[:, part], old_sb[:, part], ALU.add)
            queue = nc.sync if s % 2 == 0 else nc.scalar
            queue.dma_start(out=out[:, part], in_=total[:])
